import numpy as np
import ml_dtypes


def mxq(x, axis, fmt="e4m3"):
    dtype, down = {"e4m3": (ml_dtypes.float8_e4m3fn, 7), "e5m2": (ml_dtypes.float8_e5m2, 14)}[fmt]
    v = np.moveaxis(np.asarray(x, np.float32).astype(ml_dtypes.bfloat16).astype(np.float64), axis, -1)
    blocks = v.reshape(v.shape[:-1] + (-1, 32))
    amax = np.abs(blocks).max(-1, keepdims=True)
    byte = np.maximum(np.where(amax > 0, np.frexp(amax)[1] - 1 + 127, 0) - down, 1)
    scale = np.exp2(byte - 127.0)
    codes = (blocks / scale).astype(np.float32).astype(dtype).astype(np.float64)
    return np.moveaxis((codes * scale).reshape(v.shape), -1, axis)


WIDE = False


def mx_kscale(k):
    if not WIDE:
        return np.ones(k)
    levels = np.array([10, -10, 5, -5, 0])
    if k % 512:
        return np.exp2(np.random.permutation(np.resize(levels, k // 32))).repeat(32)
    a = np.empty((k // 512, 16))
    for p in range(k // 512):
        a[p, :8] = np.random.permutation(np.resize(levels, 8))
        for g in range(8):
            far = levels[np.abs(levels - a[p, g]) >= 10]
            a[p, g + 8] = far[np.random.randint(len(far))]
    return np.exp2(a.ravel()).repeat(32)


def f64(x):
    return np.asarray(x).astype(np.float64)


def striped(idx):
    return np.tile(idx.reshape(-1, 16).T, (8, 1)).astype(np.uint16)


def unstriped(offs):
    return offs[:16].T.reshape(-1).astype(np.int64)


def striped8(idx):
    return np.concatenate([x.reshape(-1, 16).T for x in idx]).astype(np.uint16)


def runs(offs, k):
    lists = np.stack([offs[16 * r : 16 * r + 16].T.reshape(-1) for r in range(8)]).astype(np.int64)
    return lists[np.arange(k) % 512 // 64]


def pack_weight(w):
    k, n = w.shape
    w = f64(np.asarray(w, np.float32).astype(ml_dtypes.bfloat16)).reshape(k // 32, 32, n)
    amax = np.abs(w).max(1)
    byte = np.clip(np.where(amax > 0, np.frexp(amax)[1] - 1 + 127 - 7, 1), 1, 254)
    scaled = (w * np.exp2(127.0 - byte)[:, None, :]).reshape(k, n).astype(np.float32)
    words = np.ascontiguousarray(scaled.reshape(k // 512, 128, 4, n).transpose(0, 1, 3, 2)).astype(ml_dtypes.float8_e4m3fn).view(np.uint8)
    return words, np.ascontiguousarray(byte.astype(np.uint8).reshape(k // 512, 16, n))


def unpack_weight(words, scales):
    g, p, n, _ = words.shape
    vals = np.ascontiguousarray(words).view(ml_dtypes.float8_e4m3fn).astype(np.float64) * np.repeat(np.exp2(scales.astype(np.float64) - 127.0), 8, axis=1)[..., None]
    return vals.transpose(0, 1, 3, 2).reshape(g * 512, n)


def sigmoid(v):
    return 1.0 / (1.0 + np.exp(-np.maximum(v, -700.0)))


K, T, S, N, H, G, U = 512, 1024, 512, 512, 512, 2048, 1024


def setup_inputs():
    n = np.random.standard_normal
    s = mx_kscale(K)[:, None]
    u = mx_kscale(S)
    packed_xT = pack_weight(n((K, T)) * s)
    packed_dT = pack_weight(n((K, G)) / s)
    return {
        "x_words": packed_xT[0],
        "x_scales": packed_xT[1],
        "w1": (n((K, H)) / np.sqrt(K) / s).astype(np.float32),
        "gs": (np.random.uniform(0.5, 1.5, (K, 1)) * s).astype(np.float32),
        "d_words": packed_dT[0],
        "d_scales": packed_dT[1],
        "mem": n((H, U)).astype(np.float32),
        "res": (1.5 * n((N, U))).astype(np.float32),
        "gn": (np.random.uniform(0.5, 1.5, (H, 1)) * u[:, None]).astype(np.float32),
        "w2": (n((H, N)) / np.sqrt(H) / u[:, None]).astype(np.float32),
        "offs": striped(np.random.permutation(T)[:S]),
        "n1": striped8(np.stack([np.random.permutation(S) for _ in range(8)])),
        "n2": striped8(np.stack([np.random.permutation(S) for _ in range(8)])),
        "kidx": striped8(np.random.randint(0, G, (8, H))),
        "n3": striped8(np.stack([np.random.permutation(U)[:S] for _ in range(8)])),
    }


def reference(x_words, x_scales, w1, gs, d_words, d_scales, mem, res, gn, w2, offs, n1, n2, kidx, n3):
    old = f64(mem)[np.arange(H)[:, None], runs(n3, H)]
    d_kidx = unpack_weight(d_words, d_scales)[np.arange(K)[:, None], runs(kidx, K)]
    xq = unpack_weight(x_words, x_scales)[:, unstriped(offs)]
    y = mxq(f64(w1), 0, "e4m3").T @ xq
    z = f64(gs) * (y + (sigmoid(y[np.arange(H)[:, None], runs(n1, H)])) * (y[np.arange(H)[:, None], runs(n2, H)] - y))
    s = 0.0625 * ((d_kidx.T @ mxq(z, 0, "e4m3")))
    nw = old + sigmoid(s) * (s - old)
    pg = f64(mem).copy()
    pg[np.arange(H)[:, None], runs(n3, H)] = nw
    z2 = f64(gn) * pg
    return f64(res) + (mxq(f64(w2), 0, "e4m3").T @ mxq(z2, 0, "e4m3"))

@@ -1,0 +1,255 @@
+from contextlib import ExitStack
+
+import concourse.mybir as mybir
+
+K, T, S, N, H, G, U = 512, 1024, 512, 512, 512, 2048, 1024
+FLOPS = 2 * K * H * S + 2 * K * H * S + 2 * H * N * U
+
+F32 = mybir.dt.float32
+BF16 = mybir.dt.bfloat16
+I32 = mybir.dt.int32
+U32 = mybir.dt.uint32
+U16 = mybir.dt.uint16
+U8 = mybir.dt.uint8
+FP8X4 = mybir.dt.float8_e4m3fn_x4
+ACT = mybir.ActivationFunctionType
+ALU = mybir.AluOpType
+
+P = 128
+PACK = 4
+HALF = S // 2
+LIST_COLS = S // 16
+OUT_CHUNKS = (128, 128, 256, 256, 128, 128)
+BANK = 512
+
+
+def tile_picked_pqktrackpaget_none_p_kernel(
+    tc, x_words, x_scales, w1, gs, d_words, d_scales, mem, res, gn, w2, offs, n1, n2, kidx, n3, out
+):
+    nc = tc.nc
+    with ExitStack() as ctx:
+        sb = ctx.enter_context(tc.tile_pool(name="sb", bufs=1))
+        ps = ctx.enter_context(tc.psum_pool(name="ps", bufs=1))
+
+        def tile(name, shape, dtype):
+            return sb.tile(shape, dtype, name=name, align_bytes=64)
+
+        banks = [ps.tile([P, BANK], F32, name="bank%d" % b) for b in range(8)]
+
+        def load_list(name, src):
+            lst = tile(name, [P, LIST_COLS], U16)
+            nc.sync.dma_start(lst[:], src)
+            return lst
+
+        def half_of(lst, h):
+            return lst[:, h * LIST_COLS // 2 : (h + 1) * LIST_COLS // 2]
+
+        def mx(dst, lhs_codes, lhs_scales, rhs_codes, rhs_scales):
+            nc.tensor.matmul_mx(
+                out=dst,
+                lhsT=lhs_codes.bitcast(FP8X4),
+                lhsT_scale=lhs_scales,
+                rhs=rhs_codes.bitcast(FP8X4),
+                rhs_scale=rhs_scales,
+                start=True,
+                stop=True,
+            )
+
+        x_scale_tab = tile("x_scale_tab", [P, T], U8)
+        d_scale_tab = tile("d_scale_tab", [P, G], U8)
+        nc.vector.memset(x_scale_tab[:].bitcast(I32), 0)
+        nc.vector.memset(d_scale_tab[:].bitcast(I32), 0)
+
+        offs_t = load_list("offs_t", offs)
+        x_scale_rows = x_scales[0].bitcast(I32)
+        x_scale_in = tile("x_scale_in", [P, T // 4], I32)
+        for q in range(4):
+            nc.sync.dma_start(x_scale_in[32 * q : 32 * q + 4, :], x_scale_rows[4 * q : 4 * q + 4, :])
+        x_word_tab = tile("x_word_tab", [P, T], I32)
+        nc.sync.dma_start(x_word_tab[:], x_words[0].rearrange("p c r -> p (c r)").bitcast(I32))
+        for q in range(4):
+            nc.vector.tensor_copy(x_scale_tab[32 * q : 32 * q + 4, :].bitcast(I32), x_scale_in[32 * q : 32 * q + 4, :])
+        w1_rows = w1.rearrange("(p j) c -> p j c", j=PACK)
+        w1_raw = []
+        for a in range(2):
+            raw = tile("w1_raw%d" % a, [P, PACK, H // 2], F32)
+            nc.sync.dma_start(raw[:], w1_rows[:, :, a * H // 2 : (a + 1) * H // 2])
+            w1_raw.append(raw)
+        kidx_t = load_list("kidx_t", kidx)
+        d_scale_rows = d_scales[0].bitcast(I32).rearrange("(r e) c -> e r c", e=2)
+        for e in range(2):
+            nc.sync.dma_start(d_scale_tab[e:P:16, :].bitcast(I32), d_scale_rows[e])
+        d_word_tab = tile("d_word_tab", [P, G], I32)
+        nc.sync.dma_start(d_word_tab[:], d_words[0].rearrange("p c r -> p (c r)").bitcast(I32))
+        n1_t = load_list("n1_t", n1)
+        gs_t = tile("gs_t", [P, PACK], F32)
+        nc.sync.dma_start(gs_t[:], gs.rearrange("(p t) o -> p (t o)", t=PACK))
+        n2_t = load_list("n2_t", n2)
+        w2_raw = tile("w2_raw", [P, PACK, N], F32)
+        nc.sync.dma_start(w2_raw[:], w2.rearrange("(p j) c -> p j c", j=PACK))
+        n3_t = load_list("n3_t", n3)
+        mem_rows = mem.rearrange("(p t) w -> p t w", t=PACK)
+        page = []
+        for t in range(PACK):
+            pg = tile("page%d" % t, [P, U], F32)
+            nc.sync.dma_start(pg[:], mem_rows[:, t, :])
+            page.append(pg)
+        gn_t = tile("gn_t", [P, PACK], F32)
+        nc.sync.dma_start(gn_t[:], gn.rearrange("(p t) o -> p (t o)", t=PACK))
+        res_t = tile("res_t", [P, PACK, U], F32)
+        nc.sync.dma_start(res_t[:], res.rearrange("(b p) w -> p b w", p=P))
+
+        x_codes = tile("x_codes", [P, S], U32)
+        x_sc = tile("x_sc", [P, S], U8)
+        nc.vector.tensor_copy(x_codes[:], x_word_tab[:].bitcast(U32).indirect(offs_t[:]))
+        nc.vector.tensor_copy(x_sc[:], x_scale_tab[:].indirect(offs_t[:]))
+
+        w1_bf = tile("w1_bf", [P, PACK, P, PACK], BF16)
+        for a, copy in enumerate((nc.scalar.copy, nc.vector.tensor_copy)):
+            copy(
+                w1_bf[:, :, a * P // 2 : (a + 1) * P // 2, :].rearrange("p t m j -> p m j t"),
+                w1_raw[a][:].rearrange("p j (m t) -> p m j t", t=PACK),
+            )
+        w1_codes = tile("w1_codes", [P, PACK, P], U32)
+        w1_sc = tile("w1_sc", [P, PACK, P], U8)
+        for t in range(PACK):
+            nc.vector.quantize_mx(
+                out=w1_codes[:, t, :].bitcast(FP8X4),
+                scales=w1_sc[:, t, :],
+                in_=w1_bf[:, t, :, :].rearrange("p m j -> p (m j)"),
+            )
+            mx(banks[t][:], w1_codes[:, t, :], w1_sc[:, t, :], x_codes[:], x_sc[:])
+
+        d_picked = tile("d_picked", [P, H], U32)
+        d_sc_picked = tile("d_sc_picked", [P, H], U8)
+        d_codes = tile("d_codes", [P, H], U32)
+        d_sc = tile("d_sc", [P, H], U8)
+        nc.vector.tensor_copy(d_sc_picked[:], d_scale_tab[:].indirect(kidx_t[:]))
+        nc.vector.tensor_copy(
+            d_sc[:].rearrange("p (t m) -> p m t", t=PACK), d_sc_picked[:].rearrange("p (m t) -> p m t", t=PACK)
+        )
+        for e in range(2):
+            nc.gpsimd.dma_start(d_sc[2 + e : P : 32, :].bitcast(I32), d_sc[16 + e : P : 32, :].bitcast(I32))
+        nc.vector.tensor_copy(d_picked[:], d_word_tab[:].bitcast(U32).indirect(kidx_t[:]))
+        nc.vector.tensor_copy(
+            d_codes[:].rearrange("p (t m) -> p m t", t=PACK), d_picked[:].rearrange("p (m t) -> p m t", t=PACK)
+        )
+
+        y = [tile("y%d" % t, [P, S], F32) for t in range(PACK)]
+        gy = [tile("gy%d" % t, [P, S], F32) for t in range(PACK)]
+        gate = [tile("gate%d" % h, [P, PACK, HALF], F32) for h in range(2)]
+        far = [tile("far%d" % h, [P, PACK, HALF], F32) for h in range(2)]
+        near = [tile("near%d" % h, [P, PACK, HALF], F32) for h in range(2)]
+        z_codes = tile("z_codes", [P, S], U32)
+        z_sc = tile("z_sc", [P, S], U8)
+        keep = tile("keep", [P, PACK, S], F32)
+        halves = [slice(h * HALF, (h + 1) * HALF) for h in range(2)]
+        s_banks = banks[PACK:]
+
+        def take_y(t):
+            nc.scalar.copy(y[t][:], banks[t][:])
+            nc.vector.tensor_scalar_mul(gy[t][:], y[t][:], gs_t[:, t : t + 1])
+
+        def mix(h, t):
+            nc.scalar.activation(gate[h][:, t, :], y[t][:].indirect(half_of(n1_t, h)), ACT.Sigmoid)
+            nc.vector.tensor_tensor(far[h][:, t, :], gy[t][:].indirect(half_of(n2_t, h)), gate[h][:, t, :], ALU.mult)
+            nc.vector.scalar_tensor_tensor(
+                near[h][:, t, :], gate[h][:, t, :], 1.0, gy[t][:, halves[h]], ALU.subtract, ALU.mult
+            )
+
+        def score(h):
+            cols = halves[h]
+            z_bf = tile("z_bf%d" % h, [P, HALF, PACK], BF16)
+            nc.vector.tensor_tensor(
+                z_bf[:].rearrange("p (c i) t -> p c t i", i=4),
+                far[h][:].rearrange("p t (c i) -> p c t i", i=4),
+                near[h][:].rearrange("p t (c i) -> p c t i", i=4),
+                ALU.subtract,
+            )
+            nc.vector.quantize_mx(
+                out=z_codes[:, cols].bitcast(FP8X4), scales=z_sc[:, cols], in_=z_bf[:].rearrange("p c t -> p (c t)")
+            )
+            for t in range(PACK):
+                rows = slice(t * P, (t + 1) * P)
+                mx(s_banks[t][:, cols], d_codes[:, rows], d_sc[:, rows], z_codes[:, cols], z_sc[:, cols])
+
+        def make_keep(h):
+            for t in range(PACK):
+                nc.scalar.activation(keep[:, t, halves[h]], s_banks[t][:, halves[h]], ACT.Sigmoid, scale=-0.0625)
+
+        take_y(0)
+        for t in range(PACK):
+            if t + 1 < PACK:
+                take_y(t + 1)
+            mix(0, t)
+        score(0)
+        for t in range(PACK):
+            mix(1, t)
+        make_keep(0)
+        score(1)
+
+        w2_bf = tile("w2_bf", [P, N, PACK], BF16)
+        for a in range(4):
+            cols = slice(a * P, (a + 1) * P)
+            nc.scalar.copy(
+                w2_bf[:, cols, :].rearrange("p (c i) j -> p c j i", i=4),
+                w2_raw[:, :, cols].rearrange("p j (c i) -> p c j i", i=4),
+            )
+        make_keep(1)
+
+        kept = tile("kept", [P, PACK, S], F32)
+        fresh = tile("fresh", [P, PACK, S], F32)
+        for h in range(2):
+            for t in range(PACK):
+                nc.vector.tensor_tensor(
+                    kept[:, t, halves[h]], page[t][:].indirect(half_of(n3_t, h)), keep[:, t, halves[h]], ALU.mult
+                )
+        w2_codes = tile("w2_codes", [P, N], U32)
+        w2_sc = tile("w2_sc", [P, N], U8)
+        nc.vector.quantize_mx(
+            out=w2_codes[:].bitcast(FP8X4), scales=w2_sc[:], in_=w2_bf[:].rearrange("p c j -> p (c j)")
+        )
+        for t in range(PACK):
+            nc.scalar.activation(fresh[:, t, :], s_banks[t][:], ACT.Silu, scale=0.0625)
+        z2_bf = tile("z2_bf", [P, U, PACK], BF16)
+        for t in range(PACK):
+            nc.vector.tensor_tensor(page[t][:].indirect(n3_t[:]), kept[:, t, :], fresh[:, t, :], ALU.add)
+            if t < PACK - 1:
+                nc.scalar.activation(z2_bf[:, :, t], page[t][:], ACT.Copy, scale=gn_t[:, t : t + 1])
+
+        z2_codes = tile("z2_codes", [P, U], U32)
+        z2_sc = tile("z2_sc", [P, U], U8)
+        out_rows = out.rearrange("(b p) w -> p b w", p=P)
+        last = PACK - 1
+        start = 0
+        bank_no = 0
+        for c, width in enumerate(OUT_CHUNKS):
+            cols = slice(start, start + width)
+            start = start + width
+            nc.scalar.activation(z2_bf[:, cols, last], page[last][:, cols], ACT.Copy, scale=gn_t[:, last : last + 1])
+            nc.vector.quantize_mx(
+                out=z2_codes[:, cols].bitcast(FP8X4),
+                scales=z2_sc[:, cols],
+                in_=z2_bf[:, cols, :].rearrange("p c t -> p (c t)"),
+            )
+            per_bank = BANK // width
+            for b0 in range(0, PACK, per_bank):
+                bank = banks[bank_no]
+                bank_no = bank_no + 1
+                for b in range(per_bank):
+                    rows = slice((b0 + b) * P, (b0 + b + 1) * P)
+                    mx(
+                        bank[:, b * width : (b + 1) * width],
+                        w2_codes[:, rows],
+                        w2_sc[:, rows],
+                        z2_codes[:, cols],
+                        z2_sc[:, cols],
+                    )
+                done = tile("done%d" % bank_no, [P, per_bank, width], F32)
+                nc.vector.tensor_tensor(
+                    done[:],
+                    bank[:].rearrange("p (b c) -> p b c", b=per_bank),
+                    res_t[:, b0 : b0 + per_bank, cols],
+                    ALU.add,
+                )
+                nc.sync.dma_start(out_rows[:, b0 : b0 + per_bank, cols], done[:])

@@ -17,10 +17,15 @@ ALU = mybir.AluOpType
 
 P = 128
 PACK = 4
+QUADRANT = 32
+GROUP = 16
+BANKS = 8
+BANK_COLS = 512
+LIST_COLS = S // GROUP
 HALF = S // 2
-LIST_COLS = S // 16
-OUT_CHUNKS = (128, 128, 256, 256, 128, 128)
-BANK = 512
+S_SCALE = 0.0625
+W1_LATE_ON_SCALAR = 24
+OUT_CHUNKS = (256, 256, 512)
 
 
 def tile_picked_pqktrackpaget_none_p_kernel(
@@ -31,18 +36,20 @@ def tile_picked_pqktrackpaget_none_p_kernel(
         sb = ctx.enter_context(tc.tile_pool(name="sb", bufs=1))
         ps = ctx.enter_context(tc.psum_pool(name="ps", bufs=1))
 
-        def tile(name, shape, dtype):
-            return sb.tile(shape, dtype, name=name, align_bytes=64)
+        def tile(name, shape, dtype, tag=None):
+            return sb.tile(shape, dtype, name=name, tag=tag or name, align_bytes=64)
 
-        banks = [ps.tile([P, BANK], F32, name="bank%d" % b) for b in range(8)]
+        banks = [ps.tile([P, BANK_COLS], F32, name="bank%d" % b) for b in range(BANKS)]
+        y_banks = banks[:PACK]
+        s_banks = banks[PACK:]
 
         def load_list(name, src):
-            lst = tile(name, [P, LIST_COLS], U16)
-            nc.sync.dma_start(lst[:], src)
-            return lst
+            offsets = tile(name, [P, LIST_COLS], U16)
+            nc.sync.dma_start(offsets[:], src)
+            return offsets
 
-        def half_of(lst, h):
-            return lst[:, h * LIST_COLS // 2 : (h + 1) * LIST_COLS // 2]
+        def half_of(offsets, h):
+            return offsets[:, h * LIST_COLS // 2 : (h + 1) * LIST_COLS // 2]
 
         def mx(dst, lhs_codes, lhs_scales, rhs_codes, rhs_scales):
             nc.tensor.matmul_mx(
@@ -57,18 +64,16 @@ def tile_picked_pqktrackpaget_none_p_kernel(
 
         x_scale_tab = tile("x_scale_tab", [P, T], U8)
         d_scale_tab = tile("d_scale_tab", [P, G], U8)
-        nc.vector.memset(x_scale_tab[:].bitcast(I32), 0)
         nc.vector.memset(d_scale_tab[:].bitcast(I32), 0)
+        nc.vector.memset(x_scale_tab[:].bitcast(I32), 0)
 
         offs_t = load_list("offs_t", offs)
         x_scale_rows = x_scales[0].bitcast(I32)
         x_scale_in = tile("x_scale_in", [P, T // 4], I32)
-        for q in range(4):
-            nc.sync.dma_start(x_scale_in[32 * q : 32 * q + 4, :], x_scale_rows[4 * q : 4 * q + 4, :])
+        for q in range(P // QUADRANT):
+            nc.sync.dma_start(x_scale_in[QUADRANT * q : QUADRANT * q + 4, :], x_scale_rows[4 * q : 4 * q + 4, :])
         x_word_tab = tile("x_word_tab", [P, T], I32)
         nc.sync.dma_start(x_word_tab[:], x_words[0].rearrange("p c r -> p (c r)").bitcast(I32))
-        for q in range(4):
-            nc.vector.tensor_copy(x_scale_tab[32 * q : 32 * q + 4, :].bitcast(I32), x_scale_in[32 * q : 32 * q + 4, :])
         w1_rows = w1.rearrange("(p j) c -> p j c", j=PACK)
         w1_raw = []
         for a in range(2):
@@ -78,7 +83,7 @@ def tile_picked_pqktrackpaget_none_p_kernel(
         kidx_t = load_list("kidx_t", kidx)
         d_scale_rows = d_scales[0].bitcast(I32).rearrange("(r e) c -> e r c", e=2)
         for e in range(2):
-            nc.sync.dma_start(d_scale_tab[e:P:16, :].bitcast(I32), d_scale_rows[e])
+            nc.sync.dma_start(d_scale_tab[e:P:GROUP, :].bitcast(I32), d_scale_rows[e])
         d_word_tab = tile("d_word_tab", [P, G], I32)
         nc.sync.dma_start(d_word_tab[:], d_words[0].rearrange("p c r -> p (c r)").bitcast(I32))
         n1_t = load_list("n1_t", n1)
@@ -91,25 +96,37 @@ def tile_picked_pqktrackpaget_none_p_kernel(
         mem_rows = mem.rearrange("(p t) w -> p t w", t=PACK)
         page = []
         for t in range(PACK):
-            pg = tile("page%d" % t, [P, U], F32)
-            nc.sync.dma_start(pg[:], mem_rows[:, t, :])
-            page.append(pg)
+            page_t = tile("page%d" % t, [P, U], F32)
+            nc.sync.dma_start(page_t[:], mem_rows[:, t, :])
+            page.append(page_t)
         gn_t = tile("gn_t", [P, PACK], F32)
         nc.sync.dma_start(gn_t[:], gn.rearrange("(p t) o -> p (t o)", t=PACK))
-        res_t = tile("res_t", [P, PACK, U], F32)
-        nc.sync.dma_start(res_t[:], res.rearrange("(b p) w -> p b w", p=P))
+
+        warm = tile("warm", [P, 2], F32)
+        nc.vector.memset(warm[:, 0:1], 0.0)
+        nc.scalar.activation(warm[:, 1:2], warm[:, 0:1], ACT.Sigmoid)
+        for q in range(P // QUADRANT):
+            rows = slice(QUADRANT * q, QUADRANT * q + 4)
+            nc.vector.tensor_copy(x_scale_tab[rows, :].bitcast(I32), x_scale_in[rows, :])
 
         x_codes = tile("x_codes", [P, S], U32)
         x_sc = tile("x_sc", [P, S], U8)
-        nc.vector.tensor_copy(x_codes[:], x_word_tab[:].bitcast(U32).indirect(offs_t[:]))
         nc.vector.tensor_copy(x_sc[:], x_scale_tab[:].indirect(offs_t[:]))
+        nc.vector.tensor_copy(x_codes[:], x_word_tab[:].bitcast(U32).indirect(offs_t[:]))
 
         w1_bf = tile("w1_bf", [P, PACK, P, PACK], BF16)
-        for a, copy in enumerate((nc.scalar.copy, nc.vector.tensor_copy)):
+        per_load = P // 2
+        for copy, a, m0, m1 in (
+            (nc.scalar.copy, 0, 0, per_load),
+            (nc.scalar.copy, 1, 0, W1_LATE_ON_SCALAR),
+            (nc.vector.tensor_copy, 1, W1_LATE_ON_SCALAR, per_load),
+        ):
             copy(
-                w1_bf[:, :, a * P // 2 : (a + 1) * P // 2, :].rearrange("p t m j -> p m j t"),
-                w1_raw[a][:].rearrange("p j (m t) -> p m j t", t=PACK),
+                w1_bf[:, :, a * per_load + m0 : a * per_load + m1, :].rearrange("p t m j -> p m j t"),
+                w1_raw[a][:, :, PACK * m0 : PACK * m1].rearrange("p j (m t) -> p m j t", t=PACK),
             )
+        d_sc_picked = tile("d_sc_picked", [P, H], U8)
+        nc.vector.tensor_copy(d_sc_picked[:], d_scale_tab[:].indirect(kidx_t[:]))
         w1_codes = tile("w1_codes", [P, PACK, P], U32)
         w1_sc = tile("w1_sc", [P, PACK, P], U8)
         for t in range(PACK):
@@ -118,18 +135,18 @@ def tile_picked_pqktrackpaget_none_p_kernel(
                 scales=w1_sc[:, t, :],
                 in_=w1_bf[:, t, :, :].rearrange("p m j -> p (m j)"),
             )
-            mx(banks[t][:], w1_codes[:, t, :], w1_sc[:, t, :], x_codes[:], x_sc[:])
+            mx(y_banks[t][:], w1_codes[:, t, :], w1_sc[:, t, :], x_codes[:], x_sc[:])
 
         d_picked = tile("d_picked", [P, H], U32)
-        d_sc_picked = tile("d_sc_picked", [P, H], U8)
         d_codes = tile("d_codes", [P, H], U32)
         d_sc = tile("d_sc", [P, H], U8)
-        nc.vector.tensor_copy(d_sc_picked[:], d_scale_tab[:].indirect(kidx_t[:]))
         nc.vector.tensor_copy(
-            d_sc[:].rearrange("p (t m) -> p m t", t=PACK), d_sc_picked[:].rearrange("p (m t) -> p m t", t=PACK)
+            d_sc[:].rearrange("p (t m) -> p t m", t=PACK), d_sc_picked[:].rearrange("p (m t) -> p t m", t=PACK)
         )
         for e in range(2):
-            nc.gpsimd.dma_start(d_sc[2 + e : P : 32, :].bitcast(I32), d_sc[16 + e : P : 32, :].bitcast(I32))
+            nc.sync.dma_start(
+                d_sc[2 + e : P : QUADRANT, :].bitcast(I32), d_sc[GROUP + e : P : QUADRANT, :].bitcast(I32)
+            )
         nc.vector.tensor_copy(d_picked[:], d_word_tab[:].bitcast(U32).indirect(kidx_t[:]))
         nc.vector.tensor_copy(
             d_codes[:].rearrange("p (t m) -> p m t", t=PACK), d_picked[:].rearrange("p (m t) -> p m t", t=PACK)
@@ -143,12 +160,15 @@ def tile_picked_pqktrackpaget_none_p_kernel(
         z_codes = tile("z_codes", [P, S], U32)
         z_sc = tile("z_sc", [P, S], U8)
         keep = tile("keep", [P, PACK, S], F32)
+        kept = tile("kept", [P, PACK, S], F32)
         halves = [slice(h * HALF, (h + 1) * HALF) for h in range(2)]
-        s_banks = banks[PACK:]
 
         def take_y(t):
-            nc.scalar.copy(y[t][:], banks[t][:])
-            nc.vector.tensor_scalar_mul(gy[t][:], y[t][:], gs_t[:, t : t + 1])
+            nc.scalar.copy(y[t][:], y_banks[t][:])
+            if t == 0:
+                nc.scalar.activation(gy[t][:], y_banks[t][:], ACT.Copy, scale=gs_t[:, t : t + 1])
+            else:
+                nc.vector.tensor_scalar_mul(gy[t][:], y[t][:], gs_t[:, t : t + 1])
 
         def mix(h, t):
             nc.scalar.activation(gate[h][:, t, :], y[t][:].indirect(half_of(n1_t, h)), ACT.Sigmoid)
@@ -161,35 +181,51 @@ def tile_picked_pqktrackpaget_none_p_kernel(
             cols = halves[h]
             z_bf = tile("z_bf%d" % h, [P, HALF, PACK], BF16)
             nc.vector.tensor_tensor(
-                z_bf[:].rearrange("p (c i) t -> p c t i", i=4),
-                far[h][:].rearrange("p t (c i) -> p c t i", i=4),
-                near[h][:].rearrange("p t (c i) -> p c t i", i=4),
+                z_bf[:].rearrange("p (c i) t -> p c t i", i=2),
+                far[h][:].rearrange("p t (c i) -> p c t i", i=2),
+                near[h][:].rearrange("p t (c i) -> p c t i", i=2),
                 ALU.subtract,
             )
             nc.vector.quantize_mx(
                 out=z_codes[:, cols].bitcast(FP8X4), scales=z_sc[:, cols], in_=z_bf[:].rearrange("p c t -> p (c t)")
             )
             for t in range(PACK):
-                rows = slice(t * P, (t + 1) * P)
-                mx(s_banks[t][:, cols], d_codes[:, rows], d_sc[:, rows], z_codes[:, cols], z_sc[:, cols])
+                keys = slice(t * P, (t + 1) * P)
+                mx(s_banks[t][:, cols], d_codes[:, keys], d_sc[:, keys], z_codes[:, cols], z_sc[:, cols])
 
         def make_keep(h):
             for t in range(PACK):
-                nc.scalar.activation(keep[:, t, halves[h]], s_banks[t][:, halves[h]], ACT.Sigmoid, scale=-0.0625)
+                nc.scalar.activation(keep[:, t, halves[h]], s_banks[t][:, halves[h]], ACT.Sigmoid, scale=-S_SCALE)
 
-        take_y(0)
+        def make_kept(h, t):
+            nc.vector.tensor_tensor(
+                kept[:, t, halves[h]], page[t][:].indirect(half_of(n3_t, h)), keep[:, t, halves[h]], ALU.mult
+            )
+
         for t in range(PACK):
-            if t + 1 < PACK:
-                take_y(t + 1)
+            take_y(t)
             mix(0, t)
+        mix(1, 0)
         score(0)
-        for t in range(PACK):
+        for t in range(1, PACK):
             mix(1, t)
         make_keep(0)
+        make_kept(0, 0)
         score(1)
 
+        res_rows = res.rearrange("(b p) w -> p b w", p=P)
+        first_width = OUT_CHUNKS[0]
+        first_blocks = BANK_COLS // first_width
+        res_first = []
+        for u, tag in enumerate(("near0", "gate0")):
+            part = tile("res_first%d" % u, [P, first_blocks, first_width], F32, tag=tag)
+            nc.sync.dma_start(part[:], res_rows[:, first_blocks * u : first_blocks * (u + 1), :first_width])
+            res_first.append(part)
+        res_rest = tile("res_rest", [P, PACK, U - first_width], F32, tag="far0")
+        nc.sync.dma_start(res_rest[:], res_rows[:, :, first_width:])
+
         w2_bf = tile("w2_bf", [P, N, PACK], BF16)
-        for a in range(4):
+        for a in range(N // P):
             cols = slice(a * P, (a + 1) * P)
             nc.scalar.copy(
                 w2_bf[:, cols, :].rearrange("p (c i) j -> p c j i", i=4),
@@ -197,59 +233,71 @@ def tile_picked_pqktrackpaget_none_p_kernel(
             )
         make_keep(1)
 
-        kept = tile("kept", [P, PACK, S], F32)
-        fresh = tile("fresh", [P, PACK, S], F32)
-        for h in range(2):
-            for t in range(PACK):
-                nc.vector.tensor_tensor(
-                    kept[:, t, halves[h]], page[t][:].indirect(half_of(n3_t, h)), keep[:, t, halves[h]], ALU.mult
-                )
-        w2_codes = tile("w2_codes", [P, N], U32)
+        fresh = [tile("fresh%d" % t, [P, S], F32) for t in range(PACK)]
+        for t in range(1, PACK):
+            make_kept(0, t)
+        for t in range(PACK):
+            make_kept(1, t)
+        for t in range(PACK):
+            nc.scalar.activation(fresh[t][:], s_banks[t][:], ACT.Silu, scale=S_SCALE)
+        z2_bf = tile("z2_bf", [P, U, PACK], BF16)
+        last = PACK - 1
+        for t in range(PACK):
+            nc.vector.tensor_tensor(page[t][:].indirect(n3_t[:]), kept[:, t, :], fresh[t][:], ALU.add)
+            if t < last:
+                nc.scalar.activation(z2_bf[:, :, t], page[t][:], ACT.Copy, scale=gn_t[:, t : t + 1])
+
+        w2_codes = tile("w2_codes", [P, N], U32, tag="fresh%d" % last)
         w2_sc = tile("w2_sc", [P, N], U8)
         nc.vector.quantize_mx(
             out=w2_codes[:].bitcast(FP8X4), scales=w2_sc[:], in_=w2_bf[:].rearrange("p c j -> p (c j)")
         )
-        for t in range(PACK):
-            nc.scalar.activation(fresh[:, t, :], s_banks[t][:], ACT.Silu, scale=0.0625)
-        z2_bf = tile("z2_bf", [P, U, PACK], BF16)
-        for t in range(PACK):
-            nc.vector.tensor_tensor(page[t][:].indirect(n3_t[:]), kept[:, t, :], fresh[:, t, :], ALU.add)
-            if t < PACK - 1:
-                nc.scalar.activation(z2_bf[:, :, t], page[t][:], ACT.Copy, scale=gn_t[:, t : t + 1])
-
-        z2_codes = tile("z2_codes", [P, U], U32)
         z2_sc = tile("z2_sc", [P, U], U8)
         out_rows = out.rearrange("(b p) w -> p b w", p=P)
-        last = PACK - 1
+        filled = []
+
+        def finish(g):
+            blocks, cols = filled[g]
+            count, width = blocks.stop - blocks.start, cols.stop - cols.start
+            if cols.start < first_width:
+                residual = res_first[g][:]
+            else:
+                residual = res_rest[:, blocks, cols.start - first_width : cols.stop - first_width]
+            pieces = 2 if g == BANKS - 1 else 1
+            for piece in range(pieces):
+                sub = slice(piece * width // pieces, (piece + 1) * width // pieces)
+                done = tile("done%d_%d" % (g, piece), [P, count, width // pieces], F32)
+                nc.vector.tensor_tensor(
+                    done[:], banks[g][:].rearrange("p (b c) -> p b c", b=count)[:, :, sub], residual[:, :, sub], ALU.add
+                )
+                nc.sync.dma_start(out_rows[:, blocks, cols][:, :, sub], done[:])
+
         start = 0
-        bank_no = 0
         for c, width in enumerate(OUT_CHUNKS):
             cols = slice(start, start + width)
             start = start + width
+            is_last_chunk = c == len(OUT_CHUNKS) - 1
+            if is_last_chunk:
+                finish(0)
+            z2_codes = tile("z2_codes%d" % c, [P, width], U32, tag="near0" if is_last_chunk else None)
             nc.scalar.activation(z2_bf[:, cols, last], page[last][:, cols], ACT.Copy, scale=gn_t[:, last : last + 1])
             nc.vector.quantize_mx(
-                out=z2_codes[:, cols].bitcast(FP8X4),
+                out=z2_codes[:].bitcast(FP8X4),
                 scales=z2_sc[:, cols],
                 in_=z2_bf[:, cols, :].rearrange("p c t -> p (c t)"),
             )
-            per_bank = BANK // width
-            for b0 in range(0, PACK, per_bank):
-                bank = banks[bank_no]
-                bank_no = bank_no + 1
+            per_bank = BANK_COLS // width
+            for b0 in range(0, N // P, per_bank):
+                bank = banks[len(filled)]
                 for b in range(per_bank):
-                    rows = slice((b0 + b) * P, (b0 + b + 1) * P)
+                    out_block = slice((b0 + b) * P, (b0 + b + 1) * P)
                     mx(
                         bank[:, b * width : (b + 1) * width],
-                        w2_codes[:, rows],
-                        w2_sc[:, rows],
-                        z2_codes[:, cols],
+                        w2_codes[:, out_block],
+                        w2_sc[:, out_block],
+                        z2_codes[:],
                         z2_sc[:, cols],
                     )
-                done = tile("done%d" % bank_no, [P, per_bank, width], F32)
-                nc.vector.tensor_tensor(
-                    done[:],
-                    bank[:].rearrange("p (b c) -> p b c", b=per_bank),
-                    res_t[:, b0 : b0 + per_bank, cols],
-                    ALU.add,
-                )
-                nc.sync.dma_start(out_rows[:, b0 : b0 + per_bank, cols], done[:])
+                filled.append((slice(b0, b0 + per_bank), cols))
+        for g in range(1, BANKS):
+            finish(g)

from contextlib import ExitStack

import concourse.mybir as mybir

K, T, S, N, H, G, U = 512, 1024, 512, 512, 512, 2048, 1024
FLOPS = 2 * K * H * S + 2 * K * H * S + 2 * H * N * U

F32 = mybir.dt.float32
BF16 = mybir.dt.bfloat16
I32 = mybir.dt.int32
U32 = mybir.dt.uint32
U16 = mybir.dt.uint16
U8 = mybir.dt.uint8
FP8X4 = mybir.dt.float8_e4m3fn_x4
ACT = mybir.ActivationFunctionType
ALU = mybir.AluOpType

P = 128
PACK = 4
QUADRANT = 32
GROUP = 16
BANKS = 8
BANK_COLS = 512
LIST_COLS = S // GROUP
HALF = S // 2
S_SCALE = 0.0625
W1_LATE_ON_SCALAR = 24
OUT_CHUNKS = (256, 256, 512)


def tile_picked_pqktrackpaget_none_p_kernel(
    tc, x_words, x_scales, w1, gs, d_words, d_scales, mem, res, gn, w2, offs, n1, n2, kidx, n3, out
):
    nc = tc.nc
    with ExitStack() as ctx:
        sb = ctx.enter_context(tc.tile_pool(name="sb", bufs=1))
        ps = ctx.enter_context(tc.psum_pool(name="ps", bufs=1))

        def tile(name, shape, dtype, tag=None):
            return sb.tile(shape, dtype, name=name, tag=tag or name, align_bytes=64)

        banks = [ps.tile([P, BANK_COLS], F32, name="bank%d" % b) for b in range(BANKS)]
        y_banks = banks[:PACK]
        s_banks = banks[PACK:]

        def load_list(name, src):
            offsets = tile(name, [P, LIST_COLS], U16)
            nc.sync.dma_start(offsets[:], src)
            return offsets

        def half_of(offsets, h):
            return offsets[:, h * LIST_COLS // 2 : (h + 1) * LIST_COLS // 2]

        def mx(dst, lhs_codes, lhs_scales, rhs_codes, rhs_scales):
            nc.tensor.matmul_mx(
                out=dst,
                lhsT=lhs_codes.bitcast(FP8X4),
                lhsT_scale=lhs_scales,
                rhs=rhs_codes.bitcast(FP8X4),
                rhs_scale=rhs_scales,
                start=True,
                stop=True,
            )

        x_scale_tab = tile("x_scale_tab", [P, T], U8)
        d_scale_tab = tile("d_scale_tab", [P, G], U8)
        nc.vector.memset(d_scale_tab[:].bitcast(I32), 0)
        nc.vector.memset(x_scale_tab[:].bitcast(I32), 0)

        offs_t = load_list("offs_t", offs)
        x_scale_rows = x_scales[0].bitcast(I32)
        x_scale_in = tile("x_scale_in", [P, T // 4], I32)
        for q in range(P // QUADRANT):
            nc.sync.dma_start(x_scale_in[QUADRANT * q : QUADRANT * q + 4, :], x_scale_rows[4 * q : 4 * q + 4, :])
        x_word_tab = tile("x_word_tab", [P, T], I32)
        nc.sync.dma_start(x_word_tab[:], x_words[0].rearrange("p c r -> p (c r)").bitcast(I32))
        w1_rows = w1.rearrange("(p j) c -> p j c", j=PACK)
        w1_raw = []
        for a in range(2):
            raw = tile("w1_raw%d" % a, [P, PACK, H // 2], F32)
            nc.sync.dma_start(raw[:], w1_rows[:, :, a * H // 2 : (a + 1) * H // 2])
            w1_raw.append(raw)
        kidx_t = load_list("kidx_t", kidx)
        d_scale_rows = d_scales[0].bitcast(I32).rearrange("(r e) c -> e r c", e=2)
        for e in range(2):
            nc.sync.dma_start(d_scale_tab[e:P:GROUP, :].bitcast(I32), d_scale_rows[e])
        d_word_tab = tile("d_word_tab", [P, G], I32)
        nc.sync.dma_start(d_word_tab[:], d_words[0].rearrange("p c r -> p (c r)").bitcast(I32))
        n1_t = load_list("n1_t", n1)
        gs_t = tile("gs_t", [P, PACK], F32)
        nc.sync.dma_start(gs_t[:], gs.rearrange("(p t) o -> p (t o)", t=PACK))
        n2_t = load_list("n2_t", n2)
        w2_raw = tile("w2_raw", [P, PACK, N], F32)
        nc.sync.dma_start(w2_raw[:], w2.rearrange("(p j) c -> p j c", j=PACK))
        n3_t = load_list("n3_t", n3)
        mem_rows = mem.rearrange("(p t) w -> p t w", t=PACK)
        page = []
        for t in range(PACK):
            page_t = tile("page%d" % t, [P, U], F32)
            nc.sync.dma_start(page_t[:], mem_rows[:, t, :])
            page.append(page_t)
        gn_t = tile("gn_t", [P, PACK], F32)
        nc.sync.dma_start(gn_t[:], gn.rearrange("(p t) o -> p (t o)", t=PACK))

        warm = tile("warm", [P, 2], F32)
        nc.vector.memset(warm[:, 0:1], 0.0)
        nc.scalar.activation(warm[:, 1:2], warm[:, 0:1], ACT.Sigmoid)
        for q in range(P // QUADRANT):
            rows = slice(QUADRANT * q, QUADRANT * q + 4)
            nc.vector.tensor_copy(x_scale_tab[rows, :].bitcast(I32), x_scale_in[rows, :])

        x_codes = tile("x_codes", [P, S], U32)
        x_sc = tile("x_sc", [P, S], U8)
        nc.vector.tensor_copy(x_sc[:], x_scale_tab[:].indirect(offs_t[:]))
        nc.vector.tensor_copy(x_codes[:], x_word_tab[:].bitcast(U32).indirect(offs_t[:]))

        w1_bf = tile("w1_bf", [P, PACK, P, PACK], BF16)
        per_load = P // 2
        for copy, a, m0, m1 in (
            (nc.scalar.copy, 0, 0, per_load),
            (nc.scalar.copy, 1, 0, W1_LATE_ON_SCALAR),
            (nc.vector.tensor_copy, 1, W1_LATE_ON_SCALAR, per_load),
        ):
            copy(
                w1_bf[:, :, a * per_load + m0 : a * per_load + m1, :].rearrange("p t m j -> p m j t"),
                w1_raw[a][:, :, PACK * m0 : PACK * m1].rearrange("p j (m t) -> p m j t", t=PACK),
            )
        d_sc_picked = tile("d_sc_picked", [P, H], U8)
        nc.vector.tensor_copy(d_sc_picked[:], d_scale_tab[:].indirect(kidx_t[:]))
        w1_codes = tile("w1_codes", [P, PACK, P], U32)
        w1_sc = tile("w1_sc", [P, PACK, P], U8)
        for t in range(PACK):
            nc.vector.quantize_mx(
                out=w1_codes[:, t, :].bitcast(FP8X4),
                scales=w1_sc[:, t, :],
                in_=w1_bf[:, t, :, :].rearrange("p m j -> p (m j)"),
            )
            mx(y_banks[t][:], w1_codes[:, t, :], w1_sc[:, t, :], x_codes[:], x_sc[:])

        d_picked = tile("d_picked", [P, H], U32)
        d_codes = tile("d_codes", [P, H], U32)
        d_sc = tile("d_sc", [P, H], U8)
        nc.vector.tensor_copy(
            d_sc[:].rearrange("p (t m) -> p t m", t=PACK), d_sc_picked[:].rearrange("p (m t) -> p t m", t=PACK)
        )
        for e in range(2):
            nc.sync.dma_start(
                d_sc[2 + e : P : QUADRANT, :].bitcast(I32), d_sc[GROUP + e : P : QUADRANT, :].bitcast(I32)
            )
        nc.vector.tensor_copy(d_picked[:], d_word_tab[:].bitcast(U32).indirect(kidx_t[:]))
        nc.vector.tensor_copy(
            d_codes[:].rearrange("p (t m) -> p m t", t=PACK), d_picked[:].rearrange("p (m t) -> p m t", t=PACK)
        )

        y = [tile("y%d" % t, [P, S], F32) for t in range(PACK)]
        gy = [tile("gy%d" % t, [P, S], F32) for t in range(PACK)]
        gate = [tile("gate%d" % h, [P, PACK, HALF], F32) for h in range(2)]
        far = [tile("far%d" % h, [P, PACK, HALF], F32) for h in range(2)]
        near = [tile("near%d" % h, [P, PACK, HALF], F32) for h in range(2)]
        z_codes = tile("z_codes", [P, S], U32)
        z_sc = tile("z_sc", [P, S], U8)
        keep = tile("keep", [P, PACK, S], F32)
        kept = tile("kept", [P, PACK, S], F32)
        halves = [slice(h * HALF, (h + 1) * HALF) for h in range(2)]

        def take_y(t):
            nc.scalar.copy(y[t][:], y_banks[t][:])
            if t == 0:
                nc.scalar.activation(gy[t][:], y_banks[t][:], ACT.Copy, scale=gs_t[:, t : t + 1])
            else:
                nc.vector.tensor_scalar_mul(gy[t][:], y[t][:], gs_t[:, t : t + 1])

        def mix(h, t):
            nc.scalar.activation(gate[h][:, t, :], y[t][:].indirect(half_of(n1_t, h)), ACT.Sigmoid)
            nc.vector.tensor_tensor(far[h][:, t, :], gy[t][:].indirect(half_of(n2_t, h)), gate[h][:, t, :], ALU.mult)
            nc.vector.scalar_tensor_tensor(
                near[h][:, t, :], gate[h][:, t, :], 1.0, gy[t][:, halves[h]], ALU.subtract, ALU.mult
            )

        def score(h):
            cols = halves[h]
            z_bf = tile("z_bf%d" % h, [P, HALF, PACK], BF16)
            nc.vector.tensor_tensor(
                z_bf[:].rearrange("p (c i) t -> p c t i", i=2),
                far[h][:].rearrange("p t (c i) -> p c t i", i=2),
                near[h][:].rearrange("p t (c i) -> p c t i", i=2),
                ALU.subtract,
            )
            nc.vector.quantize_mx(
                out=z_codes[:, cols].bitcast(FP8X4), scales=z_sc[:, cols], in_=z_bf[:].rearrange("p c t -> p (c t)")
            )
            for t in range(PACK):
                keys = slice(t * P, (t + 1) * P)
                mx(s_banks[t][:, cols], d_codes[:, keys], d_sc[:, keys], z_codes[:, cols], z_sc[:, cols])

        def make_keep(h):
            for t in range(PACK):
                nc.scalar.activation(keep[:, t, halves[h]], s_banks[t][:, halves[h]], ACT.Sigmoid, scale=-S_SCALE)

        def make_kept(h, t):
            nc.vector.tensor_tensor(
                kept[:, t, halves[h]], page[t][:].indirect(half_of(n3_t, h)), keep[:, t, halves[h]], ALU.mult
            )

        for t in range(PACK):
            take_y(t)
            mix(0, t)
        mix(1, 0)
        score(0)
        for t in range(1, PACK):
            mix(1, t)
        make_keep(0)
        make_kept(0, 0)
        score(1)

        res_rows = res.rearrange("(b p) w -> p b w", p=P)
        first_width = OUT_CHUNKS[0]
        first_blocks = BANK_COLS // first_width
        res_first = []
        for u, tag in enumerate(("near0", "gate0")):
            part = tile("res_first%d" % u, [P, first_blocks, first_width], F32, tag=tag)
            nc.sync.dma_start(part[:], res_rows[:, first_blocks * u : first_blocks * (u + 1), :first_width])
            res_first.append(part)
        res_rest = tile("res_rest", [P, PACK, U - first_width], F32, tag="far0")
        nc.sync.dma_start(res_rest[:], res_rows[:, :, first_width:])

        w2_bf = tile("w2_bf", [P, N, PACK], BF16)
        for a in range(N // P):
            cols = slice(a * P, (a + 1) * P)
            nc.scalar.copy(
                w2_bf[:, cols, :].rearrange("p (c i) j -> p c j i", i=4),
                w2_raw[:, :, cols].rearrange("p j (c i) -> p c j i", i=4),
            )
        make_keep(1)

        fresh = [tile("fresh%d" % t, [P, S], F32) for t in range(PACK)]
        for t in range(1, PACK):
            make_kept(0, t)
        for t in range(PACK):
            make_kept(1, t)
        for t in range(PACK):
            nc.scalar.activation(fresh[t][:], s_banks[t][:], ACT.Silu, scale=S_SCALE)
        z2_bf = tile("z2_bf", [P, U, PACK], BF16)
        last = PACK - 1
        for t in range(PACK):
            nc.vector.tensor_tensor(page[t][:].indirect(n3_t[:]), kept[:, t, :], fresh[t][:], ALU.add)
            if t < last:
                nc.scalar.activation(z2_bf[:, :, t], page[t][:], ACT.Copy, scale=gn_t[:, t : t + 1])

        w2_codes = tile("w2_codes", [P, N], U32, tag="fresh%d" % last)
        w2_sc = tile("w2_sc", [P, N], U8)
        nc.vector.quantize_mx(
            out=w2_codes[:].bitcast(FP8X4), scales=w2_sc[:], in_=w2_bf[:].rearrange("p c j -> p (c j)")
        )
        z2_sc = tile("z2_sc", [P, U], U8)
        out_rows = out.rearrange("(b p) w -> p b w", p=P)
        filled = []

        def finish(g):
            blocks, cols = filled[g]
            count, width = blocks.stop - blocks.start, cols.stop - cols.start
            if cols.start < first_width:
                residual = res_first[g][:]
            else:
                residual = res_rest[:, blocks, cols.start - first_width : cols.stop - first_width]
            pieces = 2 if g == BANKS - 1 else 1
            for piece in range(pieces):
                sub = slice(piece * width // pieces, (piece + 1) * width // pieces)
                done = tile("done%d_%d" % (g, piece), [P, count, width // pieces], F32)
                nc.vector.tensor_tensor(
                    done[:], banks[g][:].rearrange("p (b c) -> p b c", b=count)[:, :, sub], residual[:, :, sub], ALU.add
                )
                nc.sync.dma_start(out_rows[:, blocks, cols][:, :, sub], done[:])

        start = 0
        for c, width in enumerate(OUT_CHUNKS):
            cols = slice(start, start + width)
            start = start + width
            is_last_chunk = c == len(OUT_CHUNKS) - 1
            if is_last_chunk:
                finish(0)
            z2_codes = tile("z2_codes%d" % c, [P, width], U32, tag="near0" if is_last_chunk else None)
            nc.scalar.activation(z2_bf[:, cols, last], page[last][:, cols], ACT.Copy, scale=gn_t[:, last : last + 1])
            nc.vector.quantize_mx(
                out=z2_codes[:].bitcast(FP8X4),
                scales=z2_sc[:, cols],
                in_=z2_bf[:, cols, :].rearrange("p c t -> p (c t)"),
            )
            per_bank = BANK_COLS // width
            for b0 in range(0, N // P, per_bank):
                bank = banks[len(filled)]
                for b in range(per_bank):
                    out_block = slice((b0 + b) * P, (b0 + b + 1) * P)
                    mx(
                        bank[:, b * width : (b + 1) * width],
                        w2_codes[:, out_block],
                        w2_sc[:, out_block],
                        z2_codes[:],
                        z2_sc[:, cols],
                    )
                filled.append((slice(b0, b0 + per_bank), cols))
        for g in range(1, BANKS):
            finish(g)
